import numpy as np
import ml_dtypes


def mxq(x, axis, fmt="e4m3"):
    dtype, down = {"e4m3": (ml_dtypes.float8_e4m3fn, 7), "e5m2": (ml_dtypes.float8_e5m2, 14)}[fmt]
    v = np.moveaxis(np.asarray(x, np.float32).astype(ml_dtypes.bfloat16).astype(np.float64), axis, -1)
    blocks = v.reshape(v.shape[:-1] + (-1, 32))
    amax = np.abs(blocks).max(-1, keepdims=True)
    byte = np.maximum(np.where(amax > 0, np.frexp(amax)[1] - 1 + 127, 0) - down, 1)
    scale = np.exp2(byte - 127.0)
    codes = (blocks / scale).astype(np.float32).astype(dtype).astype(np.float64)
    return np.moveaxis((codes * scale).reshape(v.shape), -1, axis)


WIDE = False


def mx_kscale(k):
    if not WIDE:
        return np.ones(k)
    levels = np.array([10, -10, 5, -5, 0])
    if k % 512:
        return np.exp2(np.random.permutation(np.resize(levels, k // 32))).repeat(32)
    a = np.empty((k // 512, 16))
    for p in range(k // 512):
        a[p, :8] = np.random.permutation(np.resize(levels, 8))
        for g in range(8):
            far = levels[np.abs(levels - a[p, g]) >= 10]
            a[p, g + 8] = far[np.random.randint(len(far))]
    return np.exp2(a.ravel()).repeat(32)


BF16 = ml_dtypes.bfloat16


def bf(x):
    return np.asarray(x, np.float32).astype(BF16)


def f64(x):
    return np.asarray(x).astype(np.float64)


E2M1 = np.array([0.0, 0.5, 1.0, 1.5, 2.0, 3.0, 4.0, 6.0, -0.0, -0.5, -1.0, -1.5, -2.0, -3.0, -4.0, -6.0])


def pack_weight(w, fmt):
    k, n = w.shape
    w = f64(bf(w)).reshape(k // 32, 32, n)
    amax = np.abs(w).max(1)
    if fmt == "e4m3":
        byte = np.frexp(amax)[1] - 1 + 127 - 7
    else:
        mant, ex = np.frexp(amax / 6.0)
        byte = np.where(mant > 0.5, ex, ex - 1) + 127
    byte = np.clip(np.where(amax > 0, byte, 1), 1, 254)
    scaled = (w * np.exp2(127.0 - byte)[:, None, :]).reshape(k, n).astype(np.float32)
    by_word = np.ascontiguousarray(scaled.reshape(k // 512, 128, 4, n).transpose(0, 1, 3, 2))
    if fmt == "e4m3":
        words = by_word.astype(ml_dtypes.float8_e4m3fn).view(np.uint8)
    else:
        c = by_word.astype(ml_dtypes.float4_e2m1fn).view(np.uint8) & 0xF
        words = c[..., 0::2] | (c[..., 1::2] << 4)
    return np.ascontiguousarray(words), np.ascontiguousarray(byte.astype(np.uint8).reshape(k // 512, 16, n))


def unpack_weight(words, scales, fmt):
    g, p, n, _ = words.shape
    if fmt == "e4m3":
        vals = np.ascontiguousarray(words).view(ml_dtypes.float8_e4m3fn).astype(np.float64)
    else:
        nib = np.empty((g, p, n, 4), np.uint8)
        nib[..., 0::2] = words & 0xF
        nib[..., 1::2] = words >> 4
        vals = E2M1[nib]
    vals = vals * np.repeat(np.exp2(scales.astype(np.float64) - 127.0), 8, axis=1)[..., None]
    return vals.transpose(0, 1, 3, 2).reshape(g * 512, n)
def pack4(w):
    words, scales = pack_weight(w, "e2m1")
    return words.reshape(words.shape[0], 128, -1), scales


def unpack4(words, scales):
    return unpack_weight(words.reshape(words.shape[0], 128, -1, 2), scales, "e2m1")


def planes(Y):
    n, m = Y.shape
    b = f64(bf(Y)).reshape(n // 32, 32, m)
    amax = np.abs(b).max(1)
    byte = np.clip(np.where(amax > 0, np.frexp(amax)[1] - 1 + 127 - 7, 1), 1, 254)
    codes = (b * np.exp2(127.0 - byte)[:, None, :]).reshape(n, m).astype(np.float32).astype(ml_dtypes.float8_e4m3fn).view(np.uint8)
    words = codes.reshape(n // 512, 128, 4, m).transpose(0, 1, 3, 2)
    return np.ascontiguousarray(words), np.ascontiguousarray(byte.astype(np.uint8).reshape(n // 512, 16, m))


M, K, F, N = 1024, 1536, 2048, 1024

def setup_inputs():
    s = mx_kscale(K)
    t = mx_kscale(F)
    stock = np.random.randn(K, M) * s[:, None]
    stock_words, stock_scales = pack_weight(stock, "e4m3")
    plan = np.random.randn(K, F) / np.sqrt(K) / s[:, None] * t[None, :]
    plan_words, plan_scales = pack4(plan)
    planned = bf(0.3 * np.random.randn(F) * t)
    mix = bf(np.random.randn(F, N) * np.sqrt(2.0 / F) / t[:, None])
    balance = bf(0.3 * np.random.randn(N))
    prices = bf(np.exp(0.8 * np.random.randn(N)))
    return {"stock_words": stock_words, "stock_scales": stock_scales,
            "plan_words": plan_words, "plan_scales": plan_scales,
            "planned": planned, "mix": mix, "balance": balance, "prices": prices}

def reference(stock_words, stock_scales, plan_words, plan_scales, planned, mix, balance, prices):
    X = unpack_weight(stock_words, stock_scales, "e4m3")
    W = unpack4(plan_words, plan_scales)
    H = np.maximum((X.T @ W) + f64(planned), 0.0)
    net = mxq(H, 1, "e4m3") @ mxq(f64(mix), 0, "e4m3")
    y = (net + f64(balance)) * f64(prices)
    Y = y.T
    words, scales = planes(Y)
    return y, words, scales

@@ -1,0 +1,298 @@
+from contextlib import ExitStack
+
+import concourse.mybir as mybir
+from concourse.masks import make_identity
+
+M, K, F, N = 1024, 1536, 2048, 1024
+FLOPS = 2 * M * K * F + 2 * M * F * N
+
+F32 = mybir.dt.float32
+BF16 = mybir.dt.bfloat16
+I32 = mybir.dt.int32
+U32 = mybir.dt.uint32
+U8 = mybir.dt.uint8
+FP8X4 = mybir.dt.float8_e4m3fn_x4
+FP4X4 = mybir.dt.float4_e2m1fn_x4
+ACT = mybir.ActivationFunctionType
+ALU = mybir.AluOpType
+
+P = 128
+PACK = 4
+PASS = P * PACK
+BANK = 512
+K_PASSES = K // PASS
+F_PASSES = F // PASS
+N_GROUPS = N // PASS
+HALVES = M // BANK
+BLOCK_ROWS = 8
+QUADRANTS = 4
+
+VALUE_UNITS = [(0, 0, 512), (0, 512, 512), (1, 0, 512), (1, 512, 256), (1, 768, 256)]
+
+
+def tile_stock_transfer_value_h2_kernel(
+    tc, stock_words, stock_scales, plan_words, plan_scales, planned, mix, balance, prices, out_0, out_1, out_2
+):
+    nc = tc.nc
+
+    with ExitStack() as ctx:
+        keep = ctx.enter_context(tc.tile_pool(name="keep", bufs=1))
+        work = ctx.enter_context(tc.tile_pool(name="work", bufs=3))
+        psum = ctx.enter_context(tc.psum_pool(name="psum", bufs=8))
+        ctx.enter_context(tc.manual_schedule())
+
+        def kept(name, shape, dtype):
+            return keep.tile(shape, dtype, name=name, align_bytes=64)
+
+        def staged(name, shape, dtype):
+            return work.tile(shape, dtype, name=name, align_bytes=64)
+
+        def bank(shape, dtype):
+            return psum.tile(shape, dtype, name="bank")
+
+        x_codes = [kept("x_codes%d" % h, [P, K_PASSES, BANK], U32) for h in range(HALVES)]
+        x_scales = [kept("x_scales%d" % h, [P, K_PASSES, BANK], U8) for h in range(HALVES)]
+        w_loaded = [kept("w_loaded%d" % g, [P, K_PASSES, 2 * PASS], U8) for g in range(F_PASSES)]
+        w_scales_first = kept("w_scales_first", [P, K_PASSES, PASS], U8)
+        w_scales_rest = kept("w_scales_rest", [P, K_PASSES, F - PASS], U8)
+        w_codes = [kept("w_codes%d" % g, [P, PACK, K_PASSES, 2 * P], U8) for g in range(F_PASSES)]
+        w_scales = [kept("w_scales%d" % g, [P, PACK, K_PASSES, P], U8) for g in range(F_PASSES)]
+        v_loaded = [kept("v_loaded%d" % g, [P, PACK, N], BF16) for g in range(F_PASSES)]
+        v_codes = [[kept("v_codes%d_%d" % (g, c), [P, PASS], U32) for c in range(N_GROUPS)] for g in range(F_PASSES)]
+        v_scales = [[kept("v_scales%d_%d" % (g, c), [P, PASS], U8) for c in range(N_GROUPS)] for g in range(F_PASSES)]
+        h_codes = [[kept("h_codes%d_%d" % (g, h), [P, BANK], U32) for h in range(HALVES)] for g in range(F_PASSES)]
+        h_scales = [[kept("h_scales%d_%d" % (g, h), [P, BANK], U8) for h in range(HALVES)] for g in range(F_PASSES)]
+        y_codes = [kept("y_codes%d" % c, [P, M], U32) for c in range(N_GROUPS)]
+        y_scales = [kept("y_scales%d" % c, [P, M], U8) for c in range(N_GROUPS)]
+        ident_f32 = kept("ident_f32", [P, P], F32)
+        ident_bf16 = kept("ident_bf16", [P, P], BF16)
+        planned_rows = kept("planned_rows", [P, F_PASSES, P], BF16)
+        route_bias = kept("route_bias", [P, F_PASSES, PACK], F32)
+        balance_cols = kept("balance_cols", [P, N_GROUPS, PACK], BF16)
+        price_cols = kept("price_cols", [P, N_GROUPS, PACK], BF16)
+        price_f32 = kept("price_f32", [P, N_GROUPS, PACK], F32)
+        priced_balance = kept("priced_balance", [P, N_GROUPS, PACK], F32)
+
+        def load_scale_rows(plane, scales, cols):
+            for q in range(QUADRANTS):
+                rows = scales[:, 4 * q : 4 * q + 4, cols].rearrange("k r n -> r k n")
+                nc.sync.dma_start(out=plane[32 * q : 32 * q + 4, :, :].bitcast(I32), in_=rows.bitcast(I32))
+
+        def load_x_codes(h, passes):
+            words = stock_words.rearrange("k p m t -> p k (m t)")[:, passes, 4 * BANK * h : 4 * BANK * (h + 1)]
+            nc.sync.dma_start(out=x_codes[h][:, passes, :].bitcast(I32), in_=words.bitcast(I32))
+
+        def load_w_codes(g):
+            words = plan_words.rearrange("k p c -> p k c")[:, :, 2 * PASS * g : 2 * PASS * (g + 1)]
+            nc.sync.dma_start(out=w_loaded[g][:].bitcast(I32), in_=words.bitcast(I32))
+
+        def load_v(g):
+            rows = mix[PASS * g : PASS * (g + 1), :].rearrange("(b j r) n -> r b j n", j=PACK, r=BLOCK_ROWS)
+            for r in (0, 4, 1, 5, 2, 6, 3, 7):
+                nc.sync.dma_start(out=v_loaded[g][r:P:BLOCK_ROWS, :, :], in_=rows[r])
+
+        for plane in (w_scales_first, x_scales[0], planned_rows, w_scales_rest, x_scales[1]):
+            nc.vector.memset(plane[:].bitcast(I32), 0)
+
+        make_identity(nc, ident_f32[:])
+        nc.scalar.activation(out=ident_bf16[:], in_=ident_f32[:], func=ACT.Relu)
+
+        load_scale_rows(w_scales_first, plan_scales, slice(0, PASS))
+        load_w_codes(0)
+        load_x_codes(0, slice(0, 1))
+        load_scale_rows(x_scales[0], stock_scales, slice(0, BANK))
+        load_x_codes(0, slice(1, 2))
+        nc.sync.dma_start(
+            out=planned_rows[0:PACK, :, :].rearrange("j g (b r) -> j (g b) r", r=BLOCK_ROWS),
+            in_=planned.rearrange("(b j r) -> j b r", j=PACK, r=BLOCK_ROWS),
+        )
+        load_x_codes(0, slice(2, 3))
+        load_scale_rows(w_scales_rest, plan_scales, slice(PASS, F))
+        for g in range(1, F_PASSES):
+            load_w_codes(g)
+        nc.sync.dma_start(out=balance_cols[:], in_=balance.rearrange("(c p t) -> p c t", p=P, t=PACK))
+        nc.sync.dma_start(out=price_cols[:], in_=prices.rearrange("(c p t) -> p c t", p=P, t=PACK))
+        load_v(0)
+        load_v(1)
+        load_scale_rows(x_scales[1], stock_scales, slice(BANK, M))
+        load_x_codes(1, slice(0, K_PASSES))
+        load_v(2)
+        load_v(3)
+
+        def order_w_scales(g):
+            loaded = w_scales_first[:] if g == 0 else w_scales_rest[:, :, PASS * (g - 1) : PASS * g]
+            nc.vector.tensor_copy(
+                out=w_scales[g][:].bitcast(I32).rearrange("p j k (b w) -> p j k b w", w=2),
+                in_=loaded.bitcast(I32).rearrange("p k (b j w) -> p j k b w", j=PACK, w=2),
+            )
+
+        def order_w_codes(g):
+            nc.vector.tensor_copy(
+                out=w_codes[g][:].bitcast(I32).rearrange("p j k (b w) -> p j k b w", w=4),
+                in_=w_loaded[g][:].bitcast(I32).rearrange("p k (b j w) -> p j k b w", j=PACK, w=4),
+            )
+
+        def route_bias_to_partitions():
+            turned = bank([P, F_PASSES, P], BF16)
+            for g in range(F_PASSES):
+                nc.tensor.transpose(turned[:, g, :], planned_rows[:, g, :], ident_bf16[:])
+            nc.scalar.copy(out=route_bias[:], in_=turned[:, :, 0:PACK])
+
+        def ship_pass(acc, h, g, j, k):
+            nc.tensor.matmul_mx(
+                out=acc[:],
+                lhsT=w_codes[g][:, j, k, :].bitcast(FP4X4),
+                lhsT_scale=w_scales[g][:, j, k, :],
+                rhs=x_codes[h][:, k, :].bitcast(FP8X4),
+                rhs_scale=x_scales[h][:, k, :],
+                start=(k == 0),
+                stop=(k == K_PASSES - 1),
+            )
+
+        def ship(h, g):
+            shipped = staged("shipped", [P, PACK, BANK], BF16)
+            accs = [bank([P, BANK], F32) for j in range(PACK)]
+            pairs = [(j, k) for j in range(PACK) for k in range(K_PASSES)]
+            if (h, g) == (0, 0):
+                pairs = [(j, k) for k in range(K_PASSES) for j in range(PACK)]
+            for j, k in pairs:
+                ship_pass(accs[j], h, g, j, k)
+                if (h, g, j, k) == (0, 0, PACK - 1, 0):
+                    route_bias_to_partitions()
+                if k == K_PASSES - 1:
+                    nc.scalar.activation(
+                        out=shipped[:, j, :], in_=accs[j][:], func=ACT.Relu, bias=route_bias[:, g, j : j + 1]
+                    )
+            return shipped
+
+        def interleave(name, rows, width):
+            grouped = staged(name, [P, PACK * width], BF16)
+            nc.vector.tensor_copy(
+                out=grouped[:].rearrange("p (c i j) -> p c j i", i=4, j=PACK),
+                in_=rows.rearrange("p j (c i) -> p c j i", i=4),
+            )
+            return grouped
+
+        def interleave_v(g, c):
+            grouped = staged("v_grouped", [P, PACK * PASS], BF16)
+            nc.vector.tensor_copy(
+                out=grouped[:].rearrange("p (t m j) -> p t m j", t=PACK, j=PACK),
+                in_=v_loaded[g][:, :, PASS * c : PASS * (c + 1)].rearrange("p j (m t) -> p t m j", t=PACK),
+            )
+            return grouped
+
+        def quantize(codes, scales, grouped):
+            nc.vector.quantize_mx(out=codes.bitcast(FP8X4), scales=scales, in_=grouped[:])
+
+        def value_slot(unit, t, valued):
+            c, m0, width = unit
+            h, cols = m0 // BANK, slice(m0 % BANK, m0 % BANK + width)
+            regions = slice(P * t, P * (t + 1))
+            acc = bank([P, width], F32)
+            for g in range(F_PASSES):
+                nc.tensor.matmul_mx(
+                    out=acc[:],
+                    lhsT=v_codes[g][c][:, regions].bitcast(FP8X4),
+                    lhsT_scale=v_scales[g][c][:, regions],
+                    rhs=h_codes[g][h][:, cols].bitcast(FP8X4),
+                    rhs_scale=h_scales[g][h][:, cols],
+                    start=(g == 0),
+                    stop=(g == F_PASSES - 1),
+                )
+            nc.scalar.activation(
+                out=valued[:, t, :],
+                in_=acc[:],
+                func=ACT.Identity,
+                scale=price_f32[:, c, t : t + 1],
+                bias=priced_balance[:, c, t : t + 1],
+            )
+
+        def turn(unit, valued):
+            c, m0, width = unit
+            turned = [bank([P, PACK, P], F32) for i in range(width // P)]
+            for t in range(PACK):
+                for i in range(width // P):
+                    nc.tensor.transpose(turned[i][:, t, :], valued[:, t, P * i : P * (i + 1)], ident_f32[:])
+            return turned
+
+        def store_rows(unit, i, turned, on_vector):
+            c, m0, width = unit
+            rows = work.tile([P, PASS], F32, name="rows", bufs=6)
+            by_region = rows[:].rearrange("p (n t) -> p n t", t=PACK)
+            if on_vector:
+                nc.vector.tensor_copy(out=by_region, in_=turned[:].rearrange("p t n -> p n t"))
+            else:
+                nc.scalar.copy(out=by_region, in_=turned[:].rearrange("p t n -> p n t"))
+            nc.sync.dma_start(out=out_0[m0 + P * i : m0 + P * (i + 1), PASS * c : PASS * (c + 1)], in_=rows[:])
+
+        def store_planes(unit, grouped):
+            c, m0, width = unit
+            cols = slice(m0, m0 + width)
+            quantize(y_codes[c][:, cols], y_scales[c][:, cols], grouped)
+            words = out_1[c].rearrange("p m t -> p (m t)").bitcast(I32)
+            nc.sync.dma_start(out=words[:, cols], in_=y_codes[c][:, cols].bitcast(I32))
+            if m0 + width == M:
+                for q in range(QUADRANTS):
+                    nc.sync.dma_start(
+                        out=out_2[c, 4 * q : 4 * q + 4, :].bitcast(I32),
+                        in_=y_scales[c][32 * q : 32 * q + 4, :].bitcast(I32),
+                    )
+
+        order_w_scales(0)
+        order_w_codes(0)
+        ship_units = [(h, g) for h in range(HALVES) for g in range(F_PASSES)]
+        v_pieces = [(g, c) for c in range(N_GROUPS) for g in range(F_PASSES)]
+        for u, (h, g) in enumerate(ship_units):
+            shipped = ship(h, g)
+            if u == 0:
+                for later in range(1, F_PASSES):
+                    order_w_scales(later)
+                order_w_codes(1)
+            h_grouped = interleave("h_grouped", shipped[:], BANK)
+            if u == 0:
+                order_w_codes(2)
+                quantize(h_codes[g][h][:], h_scales[g][h][:], h_grouped)
+                order_w_codes(3)
+            elif u <= 5:
+                vg, vc = v_pieces[u - 1]
+                v_grouped = interleave_v(vg, vc)
+                quantize(h_codes[g][h][:], h_scales[g][h][:], h_grouped)
+                quantize(v_codes[vg][vc][:], v_scales[vg][vc][:], v_grouped)
+            else:
+                if u == 6:
+                    nc.vector.tensor_copy(out=price_f32[:], in_=price_cols[:])
+                else:
+                    nc.vector.tensor_tensor(out=priced_balance[:], in0=balance_cols[:], in1=price_cols[:], op=ALU.mult)
+                quantize(h_codes[g][h][:], h_scales[g][h][:], h_grouped)
+
+        late_v = v_pieces[5:]
+        previous = None
+        for u, unit in enumerate(VALUE_UNITS):
+            valued = staged("valued", [P, PACK, unit[2]], F32)
+            value_slot(unit, 0, valued)
+            if previous is not None:
+                turned = turn(previous[0], previous[1])
+                y_grouped = interleave("y_grouped", previous[1][:], previous[0][2])
+            if u == 0:
+                pending = [(piece, interleave_v(piece[0], piece[1])) for piece in late_v[:2]]
+                for (vg, vc), v_grouped in pending:
+                    quantize(v_codes[vg][vc][:], v_scales[vg][vc][:], v_grouped)
+            if u == 1:
+                vg, vc = late_v[2]
+                v_grouped = interleave_v(vg, vc)
+                store_planes(previous[0], y_grouped)
+                quantize(v_codes[vg][vc][:], v_scales[vg][vc][:], v_grouped)
+            for t in range(1, PACK):
+                if previous is not None:
+                    count = len(turned)
+                    for i in range(count * (t - 1) // 2, min(count, count * t // 2)):
+                        store_rows(previous[0], i, turned[i], u >= 2 and i % 2 == 1)
+                    if t == 1 and u >= 2:
+                        store_planes(previous[0], y_grouped)
+                value_slot(unit, t, valued)
+            previous = (unit, valued)
+        turned = turn(previous[0], previous[1])
+        y_grouped = interleave("y_grouped", previous[1][:], previous[0][2])
+        store_rows(previous[0], 0, turned[0], False)
+        store_planes(previous[0], y_grouped)
+        store_rows(previous[0], 1, turned[1], False)

@@ -27,6 +27,8 @@ HALVES = M // BANK
 BLOCK_ROWS = 8
 QUADRANTS = 4
 
+SCALE_RUNS = [(0,), (1,), (2, 3)]
+REGION_ROW = 32
 VALUE_UNITS = [(0, 0, 512), (0, 512, 512), (1, 0, 512), (1, 512, 256), (1, 768, 256)]
 
 
@@ -53,8 +55,9 @@ def tile_stock_transfer_value_h2_kernel(
         x_codes = [kept("x_codes%d" % h, [P, K_PASSES, BANK], U32) for h in range(HALVES)]
         x_scales = [kept("x_scales%d" % h, [P, K_PASSES, BANK], U8) for h in range(HALVES)]
         w_loaded = [kept("w_loaded%d" % g, [P, K_PASSES, 2 * PASS], U8) for g in range(F_PASSES)]
-        w_scales_first = kept("w_scales_first", [P, K_PASSES, PASS], U8)
-        w_scales_rest = kept("w_scales_rest", [P, K_PASSES, F - PASS], U8)
+        w_scales_loaded = [
+            kept("w_scales_loaded%d" % g, [P, K_PASSES, PASS * len(groups)], U8) for g, groups in enumerate(SCALE_RUNS)
+        ]
         w_codes = [kept("w_codes%d" % g, [P, PACK, K_PASSES, 2 * P], U8) for g in range(F_PASSES)]
         w_scales = [kept("w_scales%d" % g, [P, PACK, K_PASSES, P], U8) for g in range(F_PASSES)]
         v_loaded = [kept("v_loaded%d" % g, [P, PACK, N], BF16) for g in range(F_PASSES)]
@@ -66,12 +69,12 @@ def tile_stock_transfer_value_h2_kernel(
         y_scales = [kept("y_scales%d" % c, [P, M], U8) for c in range(N_GROUPS)]
         ident_f32 = kept("ident_f32", [P, P], F32)
         ident_bf16 = kept("ident_bf16", [P, P], BF16)
-        planned_rows = kept("planned_rows", [P, F_PASSES, P], BF16)
-        route_bias = kept("route_bias", [P, F_PASSES, PACK], F32)
-        balance_cols = kept("balance_cols", [P, N_GROUPS, PACK], BF16)
-        price_cols = kept("price_cols", [P, N_GROUPS, PACK], BF16)
-        price_f32 = kept("price_f32", [P, N_GROUPS, PACK], F32)
-        priced_balance = kept("priced_balance", [P, N_GROUPS, PACK], F32)
+        vector_rows = kept("vector_rows", [P, PASS], BF16)
+        slot_rows = kept("slot_rows", [P, PACK, P], BF16)
+        vector_cols = kept("vector_cols", [P, PACK, REGION_ROW + 2 * N_GROUPS], F32)
+        priced_balance = kept("priced_balance", [P, PACK, N_GROUPS], F32)
+        balance_at = slice(REGION_ROW, REGION_ROW + N_GROUPS)
+        price_at = slice(REGION_ROW + N_GROUPS, REGION_ROW + 2 * N_GROUPS)
 
         def load_scale_rows(plane, scales, cols):
             for q in range(QUADRANTS):
@@ -91,36 +94,39 @@ def tile_stock_transfer_value_h2_kernel(
             for r in (0, 4, 1, 5, 2, 6, 3, 7):
                 nc.sync.dma_start(out=v_loaded[g][r:P:BLOCK_ROWS, :, :], in_=rows[r])
 
-        for plane in (w_scales_first, x_scales[0], planned_rows, w_scales_rest, x_scales[1]):
+        for plane in [w_scales_loaded[0], x_scales[0], slot_rows] + w_scales_loaded[1:] + [x_scales[1]]:
             nc.vector.memset(plane[:].bitcast(I32), 0)
 
         make_identity(nc, ident_f32[:])
         nc.scalar.activation(out=ident_bf16[:], in_=ident_f32[:], func=ACT.Relu)
 
-        load_scale_rows(w_scales_first, plan_scales, slice(0, PASS))
-        load_w_codes(0)
+        nc.gpsimd.dma_start(out=vector_rows[0:F_PASSES, :], in_=planned.rearrange("(g f) -> g f", f=PASS))
+        nc.gpsimd.dma_start(out=vector_rows[balance_at, :], in_=balance.rearrange("(c n) -> c n", n=PASS))
+        nc.gpsimd.dma_start(out=vector_rows[price_at, :], in_=prices.rearrange("(c n) -> c n", n=PASS))
+
+        def load_w(run):
+            groups = SCALE_RUNS[run]
+            load_scale_rows(w_scales_loaded[run], plan_scales, slice(PASS * groups[0], PASS * (groups[-1] + 1)))
+            for g in groups:
+                load_w_codes(g)
+
+        load_w(0)
         load_x_codes(0, slice(0, 1))
         load_scale_rows(x_scales[0], stock_scales, slice(0, BANK))
         load_x_codes(0, slice(1, 2))
-        nc.sync.dma_start(
-            out=planned_rows[0:PACK, :, :].rearrange("j g (b r) -> j (g b) r", r=BLOCK_ROWS),
-            in_=planned.rearrange("(b j r) -> j b r", j=PACK, r=BLOCK_ROWS),
-        )
         load_x_codes(0, slice(2, 3))
-        load_scale_rows(w_scales_rest, plan_scales, slice(PASS, F))
-        for g in range(1, F_PASSES):
-            load_w_codes(g)
-        nc.sync.dma_start(out=balance_cols[:], in_=balance.rearrange("(c p t) -> p c t", p=P, t=PACK))
-        nc.sync.dma_start(out=price_cols[:], in_=prices.rearrange("(c p t) -> p c t", p=P, t=PACK))
+        load_w(1)
+        load_w(2)
         load_v(0)
-        load_v(1)
         load_scale_rows(x_scales[1], stock_scales, slice(BANK, M))
         load_x_codes(1, slice(0, K_PASSES))
-        load_v(2)
-        load_v(3)
+        for g in range(1, F_PASSES):
+            load_v(g)
 
         def order_w_scales(g):
-            loaded = w_scales_first[:] if g == 0 else w_scales_rest[:, :, PASS * (g - 1) : PASS * g]
+            run = min(g, len(SCALE_RUNS) - 1)
+            at = PASS * SCALE_RUNS[run].index(g)
+            loaded = w_scales_loaded[run][:, :, at : at + PASS]
             nc.vector.tensor_copy(
                 out=w_scales[g][:].bitcast(I32).rearrange("p j k (b w) -> p j k b w", w=2),
                 in_=loaded.bitcast(I32).rearrange("p k (b j w) -> p j k b w", j=PACK, w=2),
@@ -132,11 +138,17 @@ def tile_stock_transfer_value_h2_kernel(
                 in_=w_loaded[g][:].bitcast(I32).rearrange("p k (b j w) -> p j k b w", j=PACK, w=4),
             )
 
-        def route_bias_to_partitions():
-            turned = bank([P, F_PASSES, P], BF16)
-            for g in range(F_PASSES):
-                nc.tensor.transpose(turned[:, g, :], planned_rows[:, g, :], ident_bf16[:])
-            nc.scalar.copy(out=route_bias[:], in_=turned[:, :, 0:PACK])
+        def vectors_to_partitions():
+            nc.scalar.copy(
+                out=slot_rows[0:F_PASSES, :, :].rearrange("g j (b r) -> g b j r", r=BLOCK_ROWS),
+                in_=vector_rows[0:F_PASSES, :].rearrange("g (b j r) -> g b j r", j=PACK, r=BLOCK_ROWS),
+            )
+            both = slice(balance_at.start, price_at.stop)
+            nc.scalar.copy(out=slot_rows[both, :, :], in_=vector_rows[both, :].rearrange("c (p t) -> c t p", t=PACK))
+            turned = bank([P, PACK, P], BF16)
+            for slot in range(PACK):
+                nc.tensor.transpose(turned[:, slot, :], slot_rows[:, slot, :], ident_bf16[:])
+            nc.scalar.copy(out=vector_cols[:], in_=turned[:, :, 0 : price_at.stop])
 
         def ship_pass(acc, h, g, j, k):
             nc.tensor.matmul_mx(
@@ -157,12 +169,12 @@ def tile_stock_transfer_value_h2_kernel(
                 pairs = [(j, k) for k in range(K_PASSES) for j in range(PACK)]
             for j, k in pairs:
                 ship_pass(accs[j], h, g, j, k)
-                if (h, g, j, k) == (0, 0, PACK - 1, 0):
-                    route_bias_to_partitions()
-                if k == K_PASSES - 1:
-                    nc.scalar.activation(
-                        out=shipped[:, j, :], in_=accs[j][:], func=ACT.Relu, bias=route_bias[:, g, j : j + 1]
-                    )
+            if (h, g) == (0, 0):
+                vectors_to_partitions()
+            for j in range(PACK):
+                nc.scalar.activation(
+                    out=shipped[:, j, :], in_=accs[j][:], func=ACT.Relu, bias=vector_cols[:, j, g : g + 1]
+                )
             return shipped
 
         def interleave(name, rows, width):
@@ -173,13 +185,25 @@ def tile_stock_transfer_value_h2_kernel(
             )
             return grouped
 
+        def v_views(g, c, grouped):
+            return (
+                grouped[:].rearrange("p (t m j) -> p m j t", t=PACK, j=PACK),
+                v_loaded[g][:, :, PASS * c : PASS * (c + 1)].rearrange("p j (m t) -> p m j t", t=PACK),
+            )
+
         def interleave_v(g, c):
             grouped = staged("v_grouped", [P, PACK * PASS], BF16)
-            nc.vector.tensor_copy(
-                out=grouped[:].rearrange("p (t m j) -> p t m j", t=PACK, j=PACK),
-                in_=v_loaded[g][:, :, PASS * c : PASS * (c + 1)].rearrange("p j (m t) -> p t m j", t=PACK),
-            )
+            dst, src = v_views(g, c, grouped)
+            nc.vector.tensor_copy(out=dst, in_=src)
             return grouped
+
+        def interleave_v_half_on_scalar(g, c, grouped, half):
+            dst, src = v_views(g, c, grouped)
+            cols = slice(half * P // 2, (half + 1) * P // 2)
+            nc.scalar.copy(out=dst[:, cols], in_=src[:, cols])
+
+        def quantize_v(g, c, grouped):
+            quantize(v_codes[g][c][:], v_scales[g][c][:], grouped)
 
         def quantize(codes, scales, grouped):
             nc.vector.quantize_mx(out=codes.bitcast(FP8X4), scales=scales, in_=grouped[:])
@@ -203,8 +227,8 @@ def tile_stock_transfer_value_h2_kernel(
                 out=valued[:, t, :],
                 in_=acc[:],
                 func=ACT.Identity,
-                scale=price_f32[:, c, t : t + 1],
-                bias=priced_balance[:, c, t : t + 1],
+                scale=vector_cols[:, t, price_at.start + c : price_at.start + c + 1],
+                bias=priced_balance[:, t, c : c + 1],
             )
 
         def turn(unit, valued):
@@ -241,31 +265,41 @@ def tile_stock_transfer_value_h2_kernel(
         order_w_scales(0)
         order_w_codes(0)
         ship_units = [(h, g) for h in range(HALVES) for g in range(F_PASSES)]
-        v_pieces = [(g, c) for c in range(N_GROUPS) for g in range(F_PASSES)]
+        v_on_vector = {1: (0, 0), 2: (0, 1), 3: (1, 0), 4: (2, 0), 5: (3, 0)}
+        v_on_scalar = {4: (1, 1), 6: (2, 1)}
         for u, (h, g) in enumerate(ship_units):
             shipped = ship(h, g)
             if u == 0:
-                for later in range(1, F_PASSES):
-                    order_w_scales(later)
+                order_w_scales(1)
                 order_w_codes(1)
+                order_w_scales(2)
+                order_w_codes(2)
+            if u in v_on_scalar:
+                scalar_piece = v_on_scalar[u]
+                scalar_grouped = work.tile([P, PACK * PASS], BF16, name="v_grouped_scalar", bufs=2, align_bytes=64)
+            if u >= 4:
+                interleave_v_half_on_scalar(scalar_piece[0], scalar_piece[1], scalar_grouped, u % 2)
             h_grouped = interleave("h_grouped", shipped[:], BANK)
             if u == 0:
-                order_w_codes(2)
-                quantize(h_codes[g][h][:], h_scales[g][h][:], h_grouped)
+                order_w_scales(3)
                 order_w_codes(3)
-            elif u <= 5:
-                vg, vc = v_pieces[u - 1]
+                quantize(h_codes[g][h][:], h_scales[g][h][:], h_grouped)
+            elif u in v_on_vector:
+                vg, vc = v_on_vector[u]
                 v_grouped = interleave_v(vg, vc)
                 quantize(h_codes[g][h][:], h_scales[g][h][:], h_grouped)
-                quantize(v_codes[vg][vc][:], v_scales[vg][vc][:], v_grouped)
-            else:
-                if u == 6:
-                    nc.vector.tensor_copy(out=price_f32[:], in_=price_cols[:])
-                else:
-                    nc.vector.tensor_tensor(out=priced_balance[:], in0=balance_cols[:], in1=price_cols[:], op=ALU.mult)
+                quantize_v(vg, vc, v_grouped)
+            elif u == 6:
+                quantize_v(1, 1, first_scalar_grouped)
                 quantize(h_codes[g][h][:], h_scales[g][h][:], h_grouped)
+            else:
+                nc.vector.tensor_tensor(
+                    out=priced_balance[:], in0=vector_cols[:, :, balance_at], in1=vector_cols[:, :, price_at], op=ALU.mult
+                )
+                quantize(h_codes[g][h][:], h_scales[g][h][:], h_grouped)
+            if u == 5:
+                first_scalar_grouped = scalar_grouped
 
-        late_v = v_pieces[5:]
         previous = None
         for u, unit in enumerate(VALUE_UNITS):
             valued = staged("valued", [P, PACK, unit[2]], F32)
@@ -274,20 +308,15 @@ def tile_stock_transfer_value_h2_kernel(
                 turned = turn(previous[0], previous[1])
                 y_grouped = interleave("y_grouped", previous[1][:], previous[0][2])
             if u == 0:
-                pending = [(piece, interleave_v(piece[0], piece[1])) for piece in late_v[:2]]
-                for (vg, vc), v_grouped in pending:
-                    quantize(v_codes[vg][vc][:], v_scales[vg][vc][:], v_grouped)
-            if u == 1:
-                vg, vc = late_v[2]
-                v_grouped = interleave_v(vg, vc)
-                store_planes(previous[0], y_grouped)
-                quantize(v_codes[vg][vc][:], v_scales[vg][vc][:], v_grouped)
+                v_grouped = interleave_v(3, 1)
+                quantize_v(2, 1, scalar_grouped)
+                quantize_v(3, 1, v_grouped)
             for t in range(1, PACK):
                 if previous is not None:
                     count = len(turned)
                     for i in range(count * (t - 1) // 2, min(count, count * t // 2)):
-                        store_rows(previous[0], i, turned[i], u >= 2 and i % 2 == 1)
-                    if t == 1 and u >= 2:
+                        store_rows(previous[0], i, turned[i], i % 2 == 1)
+                    if t == 1:
                         store_planes(previous[0], y_grouped)
                 value_slot(unit, t, valued)
             previous = (unit, valued)

from contextlib import ExitStack

import concourse.mybir as mybir
from concourse.masks import make_identity

M, K, F, N = 1024, 1536, 2048, 1024
FLOPS = 2 * M * K * F + 2 * M * F * N

F32 = mybir.dt.float32
BF16 = mybir.dt.bfloat16
I32 = mybir.dt.int32
U32 = mybir.dt.uint32
U8 = mybir.dt.uint8
FP8X4 = mybir.dt.float8_e4m3fn_x4
FP4X4 = mybir.dt.float4_e2m1fn_x4
ACT = mybir.ActivationFunctionType
ALU = mybir.AluOpType

P = 128
PACK = 4
PASS = P * PACK
BANK = 512
K_PASSES = K // PASS
F_PASSES = F // PASS
N_GROUPS = N // PASS
HALVES = M // BANK
BLOCK_ROWS = 8
QUADRANTS = 4

SCALE_RUNS = [(0,), (1,), (2, 3)]
REGION_ROW = 32
VALUE_UNITS = [(0, 0, 512), (0, 512, 512), (1, 0, 512), (1, 512, 256), (1, 768, 256)]


def tile_stock_transfer_value_h2_kernel(
    tc, stock_words, stock_scales, plan_words, plan_scales, planned, mix, balance, prices, out_0, out_1, out_2
):
    nc = tc.nc

    with ExitStack() as ctx:
        keep = ctx.enter_context(tc.tile_pool(name="keep", bufs=1))
        work = ctx.enter_context(tc.tile_pool(name="work", bufs=3))
        psum = ctx.enter_context(tc.psum_pool(name="psum", bufs=8))
        ctx.enter_context(tc.manual_schedule())

        def kept(name, shape, dtype):
            return keep.tile(shape, dtype, name=name, align_bytes=64)

        def staged(name, shape, dtype):
            return work.tile(shape, dtype, name=name, align_bytes=64)

        def bank(shape, dtype):
            return psum.tile(shape, dtype, name="bank")

        x_codes = [kept("x_codes%d" % h, [P, K_PASSES, BANK], U32) for h in range(HALVES)]
        x_scales = [kept("x_scales%d" % h, [P, K_PASSES, BANK], U8) for h in range(HALVES)]
        w_loaded = [kept("w_loaded%d" % g, [P, K_PASSES, 2 * PASS], U8) for g in range(F_PASSES)]
        w_scales_loaded = [
            kept("w_scales_loaded%d" % g, [P, K_PASSES, PASS * len(groups)], U8) for g, groups in enumerate(SCALE_RUNS)
        ]
        w_codes = [kept("w_codes%d" % g, [P, PACK, K_PASSES, 2 * P], U8) for g in range(F_PASSES)]
        w_scales = [kept("w_scales%d" % g, [P, PACK, K_PASSES, P], U8) for g in range(F_PASSES)]
        v_loaded = [kept("v_loaded%d" % g, [P, PACK, N], BF16) for g in range(F_PASSES)]
        v_codes = [[kept("v_codes%d_%d" % (g, c), [P, PASS], U32) for c in range(N_GROUPS)] for g in range(F_PASSES)]
        v_scales = [[kept("v_scales%d_%d" % (g, c), [P, PASS], U8) for c in range(N_GROUPS)] for g in range(F_PASSES)]
        h_codes = [[kept("h_codes%d_%d" % (g, h), [P, BANK], U32) for h in range(HALVES)] for g in range(F_PASSES)]
        h_scales = [[kept("h_scales%d_%d" % (g, h), [P, BANK], U8) for h in range(HALVES)] for g in range(F_PASSES)]
        y_codes = [kept("y_codes%d" % c, [P, M], U32) for c in range(N_GROUPS)]
        y_scales = [kept("y_scales%d" % c, [P, M], U8) for c in range(N_GROUPS)]
        ident_f32 = kept("ident_f32", [P, P], F32)
        ident_bf16 = kept("ident_bf16", [P, P], BF16)
        vector_rows = kept("vector_rows", [P, PASS], BF16)
        slot_rows = kept("slot_rows", [P, PACK, P], BF16)
        vector_cols = kept("vector_cols", [P, PACK, REGION_ROW + 2 * N_GROUPS], F32)
        priced_balance = kept("priced_balance", [P, PACK, N_GROUPS], F32)
        balance_at = slice(REGION_ROW, REGION_ROW + N_GROUPS)
        price_at = slice(REGION_ROW + N_GROUPS, REGION_ROW + 2 * N_GROUPS)

        def load_scale_rows(plane, scales, cols):
            for q in range(QUADRANTS):
                rows = scales[:, 4 * q : 4 * q + 4, cols].rearrange("k r n -> r k n")
                nc.sync.dma_start(out=plane[32 * q : 32 * q + 4, :, :].bitcast(I32), in_=rows.bitcast(I32))

        def load_x_codes(h, passes):
            words = stock_words.rearrange("k p m t -> p k (m t)")[:, passes, 4 * BANK * h : 4 * BANK * (h + 1)]
            nc.sync.dma_start(out=x_codes[h][:, passes, :].bitcast(I32), in_=words.bitcast(I32))

        def load_w_codes(g):
            words = plan_words.rearrange("k p c -> p k c")[:, :, 2 * PASS * g : 2 * PASS * (g + 1)]
            nc.sync.dma_start(out=w_loaded[g][:].bitcast(I32), in_=words.bitcast(I32))

        def load_v(g):
            rows = mix[PASS * g : PASS * (g + 1), :].rearrange("(b j r) n -> r b j n", j=PACK, r=BLOCK_ROWS)
            for r in (0, 4, 1, 5, 2, 6, 3, 7):
                nc.sync.dma_start(out=v_loaded[g][r:P:BLOCK_ROWS, :, :], in_=rows[r])

        for plane in [w_scales_loaded[0], x_scales[0], slot_rows] + w_scales_loaded[1:] + [x_scales[1]]:
            nc.vector.memset(plane[:].bitcast(I32), 0)

        make_identity(nc, ident_f32[:])
        nc.scalar.activation(out=ident_bf16[:], in_=ident_f32[:], func=ACT.Relu)

        nc.gpsimd.dma_start(out=vector_rows[0:F_PASSES, :], in_=planned.rearrange("(g f) -> g f", f=PASS))
        nc.gpsimd.dma_start(out=vector_rows[balance_at, :], in_=balance.rearrange("(c n) -> c n", n=PASS))
        nc.gpsimd.dma_start(out=vector_rows[price_at, :], in_=prices.rearrange("(c n) -> c n", n=PASS))

        def load_w(run):
            groups = SCALE_RUNS[run]
            load_scale_rows(w_scales_loaded[run], plan_scales, slice(PASS * groups[0], PASS * (groups[-1] + 1)))
            for g in groups:
                load_w_codes(g)

        load_w(0)
        load_x_codes(0, slice(0, 1))
        load_scale_rows(x_scales[0], stock_scales, slice(0, BANK))
        load_x_codes(0, slice(1, 2))
        load_x_codes(0, slice(2, 3))
        load_w(1)
        load_w(2)
        load_v(0)
        load_scale_rows(x_scales[1], stock_scales, slice(BANK, M))
        load_x_codes(1, slice(0, K_PASSES))
        for g in range(1, F_PASSES):
            load_v(g)

        def order_w_scales(g):
            run = min(g, len(SCALE_RUNS) - 1)
            at = PASS * SCALE_RUNS[run].index(g)
            loaded = w_scales_loaded[run][:, :, at : at + PASS]
            nc.vector.tensor_copy(
                out=w_scales[g][:].bitcast(I32).rearrange("p j k (b w) -> p j k b w", w=2),
                in_=loaded.bitcast(I32).rearrange("p k (b j w) -> p j k b w", j=PACK, w=2),
            )

        def order_w_codes(g):
            nc.vector.tensor_copy(
                out=w_codes[g][:].bitcast(I32).rearrange("p j k (b w) -> p j k b w", w=4),
                in_=w_loaded[g][:].bitcast(I32).rearrange("p k (b j w) -> p j k b w", j=PACK, w=4),
            )

        def vectors_to_partitions():
            nc.scalar.copy(
                out=slot_rows[0:F_PASSES, :, :].rearrange("g j (b r) -> g b j r", r=BLOCK_ROWS),
                in_=vector_rows[0:F_PASSES, :].rearrange("g (b j r) -> g b j r", j=PACK, r=BLOCK_ROWS),
            )
            both = slice(balance_at.start, price_at.stop)
            nc.scalar.copy(out=slot_rows[both, :, :], in_=vector_rows[both, :].rearrange("c (p t) -> c t p", t=PACK))
            turned = bank([P, PACK, P], BF16)
            for slot in range(PACK):
                nc.tensor.transpose(turned[:, slot, :], slot_rows[:, slot, :], ident_bf16[:])
            nc.scalar.copy(out=vector_cols[:], in_=turned[:, :, 0 : price_at.stop])

        def ship_pass(acc, h, g, j, k):
            nc.tensor.matmul_mx(
                out=acc[:],
                lhsT=w_codes[g][:, j, k, :].bitcast(FP4X4),
                lhsT_scale=w_scales[g][:, j, k, :],
                rhs=x_codes[h][:, k, :].bitcast(FP8X4),
                rhs_scale=x_scales[h][:, k, :],
                start=(k == 0),
                stop=(k == K_PASSES - 1),
            )

        def ship(h, g):
            shipped = staged("shipped", [P, PACK, BANK], BF16)
            accs = [bank([P, BANK], F32) for j in range(PACK)]
            pairs = [(j, k) for j in range(PACK) for k in range(K_PASSES)]
            if (h, g) == (0, 0):
                pairs = [(j, k) for k in range(K_PASSES) for j in range(PACK)]
            for j, k in pairs:
                ship_pass(accs[j], h, g, j, k)
            if (h, g) == (0, 0):
                vectors_to_partitions()
            for j in range(PACK):
                nc.scalar.activation(
                    out=shipped[:, j, :], in_=accs[j][:], func=ACT.Relu, bias=vector_cols[:, j, g : g + 1]
                )
            return shipped

        def interleave(name, rows, width):
            grouped = staged(name, [P, PACK * width], BF16)
            nc.vector.tensor_copy(
                out=grouped[:].rearrange("p (c i j) -> p c j i", i=4, j=PACK),
                in_=rows.rearrange("p j (c i) -> p c j i", i=4),
            )
            return grouped

        def v_views(g, c, grouped):
            return (
                grouped[:].rearrange("p (t m j) -> p m j t", t=PACK, j=PACK),
                v_loaded[g][:, :, PASS * c : PASS * (c + 1)].rearrange("p j (m t) -> p m j t", t=PACK),
            )

        def interleave_v(g, c):
            grouped = staged("v_grouped", [P, PACK * PASS], BF16)
            dst, src = v_views(g, c, grouped)
            nc.vector.tensor_copy(out=dst, in_=src)
            return grouped

        def interleave_v_half_on_scalar(g, c, grouped, half):
            dst, src = v_views(g, c, grouped)
            cols = slice(half * P // 2, (half + 1) * P // 2)
            nc.scalar.copy(out=dst[:, cols], in_=src[:, cols])

        def quantize_v(g, c, grouped):
            quantize(v_codes[g][c][:], v_scales[g][c][:], grouped)

        def quantize(codes, scales, grouped):
            nc.vector.quantize_mx(out=codes.bitcast(FP8X4), scales=scales, in_=grouped[:])

        def value_slot(unit, t, valued):
            c, m0, width = unit
            h, cols = m0 // BANK, slice(m0 % BANK, m0 % BANK + width)
            regions = slice(P * t, P * (t + 1))
            acc = bank([P, width], F32)
            for g in range(F_PASSES):
                nc.tensor.matmul_mx(
                    out=acc[:],
                    lhsT=v_codes[g][c][:, regions].bitcast(FP8X4),
                    lhsT_scale=v_scales[g][c][:, regions],
                    rhs=h_codes[g][h][:, cols].bitcast(FP8X4),
                    rhs_scale=h_scales[g][h][:, cols],
                    start=(g == 0),
                    stop=(g == F_PASSES - 1),
                )
            nc.scalar.activation(
                out=valued[:, t, :],
                in_=acc[:],
                func=ACT.Identity,
                scale=vector_cols[:, t, price_at.start + c : price_at.start + c + 1],
                bias=priced_balance[:, t, c : c + 1],
            )

        def turn(unit, valued):
            c, m0, width = unit
            turned = [bank([P, PACK, P], F32) for i in range(width // P)]
            for t in range(PACK):
                for i in range(width // P):
                    nc.tensor.transpose(turned[i][:, t, :], valued[:, t, P * i : P * (i + 1)], ident_f32[:])
            return turned

        def store_rows(unit, i, turned, on_vector):
            c, m0, width = unit
            rows = work.tile([P, PASS], F32, name="rows", bufs=6)
            by_region = rows[:].rearrange("p (n t) -> p n t", t=PACK)
            if on_vector:
                nc.vector.tensor_copy(out=by_region, in_=turned[:].rearrange("p t n -> p n t"))
            else:
                nc.scalar.copy(out=by_region, in_=turned[:].rearrange("p t n -> p n t"))
            nc.sync.dma_start(out=out_0[m0 + P * i : m0 + P * (i + 1), PASS * c : PASS * (c + 1)], in_=rows[:])

        def store_planes(unit, grouped):
            c, m0, width = unit
            cols = slice(m0, m0 + width)
            quantize(y_codes[c][:, cols], y_scales[c][:, cols], grouped)
            words = out_1[c].rearrange("p m t -> p (m t)").bitcast(I32)
            nc.sync.dma_start(out=words[:, cols], in_=y_codes[c][:, cols].bitcast(I32))
            if m0 + width == M:
                for q in range(QUADRANTS):
                    nc.sync.dma_start(
                        out=out_2[c, 4 * q : 4 * q + 4, :].bitcast(I32),
                        in_=y_scales[c][32 * q : 32 * q + 4, :].bitcast(I32),
                    )

        order_w_scales(0)
        order_w_codes(0)
        ship_units = [(h, g) for h in range(HALVES) for g in range(F_PASSES)]
        v_on_vector = {1: (0, 0), 2: (0, 1), 3: (1, 0), 4: (2, 0), 5: (3, 0)}
        v_on_scalar = {4: (1, 1), 6: (2, 1)}
        for u, (h, g) in enumerate(ship_units):
            shipped = ship(h, g)
            if u == 0:
                order_w_scales(1)
                order_w_codes(1)
                order_w_scales(2)
                order_w_codes(2)
            if u in v_on_scalar:
                scalar_piece = v_on_scalar[u]
                scalar_grouped = work.tile([P, PACK * PASS], BF16, name="v_grouped_scalar", bufs=2, align_bytes=64)
            if u >= 4:
                interleave_v_half_on_scalar(scalar_piece[0], scalar_piece[1], scalar_grouped, u % 2)
            h_grouped = interleave("h_grouped", shipped[:], BANK)
            if u == 0:
                order_w_scales(3)
                order_w_codes(3)
                quantize(h_codes[g][h][:], h_scales[g][h][:], h_grouped)
            elif u in v_on_vector:
                vg, vc = v_on_vector[u]
                v_grouped = interleave_v(vg, vc)
                quantize(h_codes[g][h][:], h_scales[g][h][:], h_grouped)
                quantize_v(vg, vc, v_grouped)
            elif u == 6:
                quantize_v(1, 1, first_scalar_grouped)
                quantize(h_codes[g][h][:], h_scales[g][h][:], h_grouped)
            else:
                nc.vector.tensor_tensor(
                    out=priced_balance[:], in0=vector_cols[:, :, balance_at], in1=vector_cols[:, :, price_at], op=ALU.mult
                )
                quantize(h_codes[g][h][:], h_scales[g][h][:], h_grouped)
            if u == 5:
                first_scalar_grouped = scalar_grouped

        previous = None
        for u, unit in enumerate(VALUE_UNITS):
            valued = staged("valued", [P, PACK, unit[2]], F32)
            value_slot(unit, 0, valued)
            if previous is not None:
                turned = turn(previous[0], previous[1])
                y_grouped = interleave("y_grouped", previous[1][:], previous[0][2])
            if u == 0:
                v_grouped = interleave_v(3, 1)
                quantize_v(2, 1, scalar_grouped)
                quantize_v(3, 1, v_grouped)
            for t in range(1, PACK):
                if previous is not None:
                    count = len(turned)
                    for i in range(count * (t - 1) // 2, min(count, count * t // 2)):
                        store_rows(previous[0], i, turned[i], i % 2 == 1)
                    if t == 1:
                        store_planes(previous[0], y_grouped)
                value_slot(unit, t, valued)
            previous = (unit, valued)
        turned = turn(previous[0], previous[1])
        y_grouped = interleave("y_grouped", previous[1][:], previous[0][2])
        store_rows(previous[0], 0, turned[0], False)
        store_planes(previous[0], y_grouped)
        store_rows(previous[0], 1, turned[1], False)
